import numpy as np
CORES = [89,94,345,350]
N = 4
TK = 256
NT = N * TK
EPS = 0.01
def setup_inputs(rng):
    x = (rng.standard_normal((N, 128, TK), dtype=np.float32) * (0.5 + np.arange(N, dtype=np.float32).reshape(N, 1, 1) / N) + rng.standard_normal((N, 128, 1), dtype=np.float32))
    return {"x": x}
def reference(x):
    X = x.astype(np.float64)
    mu = X.sum(axis=(0, 2)).reshape(1, 128, 1) / NT
    rs = 1.0 / np.sqrt(((X - mu) ** 2).sum(axis=(0, 2)).reshape(1, 128, 1) / NT + EPS)
    n = (X - mu) * rs
    return {"y": n.astype(np.float32)}

@@ -1,0 +1,130 @@
+from concourse.bass import DstId, RemoteDMATransfer
+from concourse.mybir import AluOpType, AxisListType, ActivationFunctionType
+
+TK = 256
+NT = 4 * TK
+EPS = 0.01
+SIM_CORES = 512
+
+K_SEND = 4
+K_RELAY = 8
+
+SCRATCH = {
+    "xs": ("sbuf", [128, TK], "float32"),
+    "xc": ("sbuf", [128, TK], "float32"),
+    "st": ("sbuf", [128, 4], "float32"),
+    "part": ("sbuf", [128, 4], "float32"),
+    "rem": ("sbuf", [128, 4], "float32"),
+    "rl": ("sbuf", [128, 4], "float32"),
+    "pre": ("sbuf", [128, 4], "float32"),
+    "fin": ("sbuf", [128, 8], "float32"),
+}
+SEMAPHORES = ["ld", "stt", "pa", "ra", "rla", "snt", "pr", "f1", "mu", "cen", "sd", "rs", "fy", "sto"]
+
+
+def _engines(allowed, k):
+    bits = [b for b in range(allowed.bit_length()) if (allowed >> b) & 1]
+    m = 0
+    for b in bits[:k]:
+        m |= 1 << b
+    return m
+
+
+def _plan(T, topo):
+    per_host = topo.CORES_PER_HOST
+    groups = {}
+    for c in T.cores:
+        groups.setdefault(topo.host(c), []).append(c)
+    relays = {}
+    for hs, snd in groups.items():
+        for hd, rcv in groups.items():
+            if hd == hs:
+                continue
+            place = snd[0] % per_host
+            cands = [h * per_host + place for h in range(SIM_CORES // per_host) if h not in groups]
+            cands = [c for c in cands
+                     if all(topo.may_write(s, c) for s in snd) and all(topo.may_write(c, d) for d in rcv)]
+            cands.sort(key=lambda c: topo.rack(topo.host(c)) != topo.rack(hs))
+            relays[cands[0]] = (snd, rcv)
+    return relays
+
+
+def _relay_program(g, core, T, topo, snd, rcv):
+    allowed = topo.mask(core, rcv[0])
+    for d in rcv:
+        allowed &= topo.mask(core, d)
+    ids = []
+    for d in rcv:
+        rid, pid = topo.addr(d, core)
+        ids.append(DstId(rid=rid, pnc=pid))
+    g.wait_ge(T.sem.rla, K_SEND * len(snd))
+    g.remote_dma_fused(
+        [RemoteDMATransfer(dst_ids=ids, dma_engine_mask=_engines(allowed, K_RELAY), remote_sem=T.sem.ra,
+                           srcs=[T.rl[:, 2 * i:2 * i + 2] for i in range(len(snd))],
+                           dsts=[T.rem[:, 0:2] for _ in rcv], alu_op=1)],
+        local_sem=T.sem.snt)
+    g.wait_ge(T.sem.snt, K_RELAY)
+
+
+def rank_program(g, core, T, topo):
+    relays = _plan(T, topo)
+    if core in relays:
+        _relay_program(g, core, T, topo, *relays[core])
+        return
+    if T.rank_of(core) is None:
+        return
+    V, S, Y, sem = g.vector, g.scalar, g.sync, T.sem
+    A, F = AluOpType, ActivationFunctionType
+    relay, slot = [(r, sr[0].index(core)) for r, sr in relays.items() if core in sr[0]][0]
+    partner = [c for c in T.cores if c != core and topo.host(c) == topo.host(core) and topo.chip(c) == topo.chip(core)][0]
+    st, part, rem, pre, fin, xs, xc = T.st, T.part, T.rem, T.pre, T.fin, T.xs, T.xc
+    e2, mu, musq, sd, rs = (fin[:, i:i + 1] for i in range(5))
+    half = TK // 2
+
+    Y.dma_start(xs[:], T.x[:]).then_inc(sem.ld, 16)
+    V.wait_ge(sem.ld, 16)
+    V.tensor_reduce(out=st[:, 0:1], in_=xs[:], axis=AxisListType.X, op=A.add).then_inc(sem.stt, 1)
+    S.wait_ge(sem.ld, 16)
+    S.activation(out=xc[:], in_=xs[:], func=F.Square, accum_out=st[:, 1:2]).then_inc(sem.stt, 1)
+
+    g.wait_ge(sem.stt, 2)
+    rid, pid = topo.addr(relay, core)
+    g.remote_dma(T.rl[:, 2 * slot:2 * slot + 2], st[:, 0:2], sem.rla, sem.snt, pid, rid,
+                 _engines(topo.mask(core, relay), K_SEND))
+    rid, pid = topo.addr(partner, core)
+    g.remote_dma(part[:, 0:2], st[:, 0:2], sem.pa, sem.snt, pid, rid,
+                 _engines(topo.mask(core, partner) & topo.mask(core, relay), K_SEND))
+
+    V.wait_ge(sem.stt, 2)
+    V.wait_ge(sem.pa, K_SEND)
+    V.tensor_tensor(out=pre[:, 0:2], in0=st[:, 0:2], in1=part[:, 0:2], op=A.add).then_inc(sem.pr, 1)
+    V.wait_ge(sem.pr, 1)
+    V.tensor_scalar(out=pre[:, 2:3], in0=pre[:, 0:1], scalar1=1.0 / NT, scalar2=None, op0=A.mult).then_inc(sem.pr, 1)
+    V.tensor_scalar(out=pre[:, 3:4], in0=pre[:, 1:2], scalar1=NT * EPS, scalar2=None, op0=A.add).then_inc(sem.pr, 1)
+    V.wait_ge(sem.pr, 3)
+    S.wait_ge(sem.pr, 3)
+
+    S.wait_ge(sem.ra, K_RELAY)
+    S.activation(out=musq, in_=rem[:, 0:1], func=F.Square, bias=pre[:, 2:3], scale=1.0 / NT).then_inc(sem.f1, 1)
+    V.wait_ge(sem.ra, K_RELAY)
+    V.tensor_scalar(out=e2, in0=rem[:, 1:2], scalar1=pre[:, 3:4], scalar2=1.0 / NT,
+                    op0=A.add, op1=A.mult).then_inc(sem.f1, 1)
+    V.tensor_scalar(out=mu, in0=rem[:, 0:1], scalar1=pre[:, 0:1], scalar2=1.0 / NT,
+                    op0=A.add, op1=A.mult).then_inc(sem.mu, 1)
+    S.wait_ge(sem.f1, 2)
+    S.activation(out=sd, in_=musq, func=F.Sqrt, bias=e2, scale=-1.0).then_inc(sem.sd, 1)
+    V.wait_ge(sem.mu, 1)
+    V.tensor_scalar(out=xc[:], in0=xs[:], scalar1=mu, scalar2=None, op0=A.subtract).then_inc(sem.cen, 1)
+    V.wait_ge(sem.sd, 1)
+    V.reciprocal(out=rs, in_=sd).then_inc(sem.rs, 1)
+    V.wait_ge(sem.rs, 1)
+    V.wait_ge(sem.cen, 1)
+    V.tensor_scalar(out=xc[:, 0:half], in0=xc[:, 0:half], scalar1=rs, scalar2=None, op0=A.mult).then_inc(sem.fy, 1)
+    S.wait_ge(sem.rs, 1)
+    S.wait_ge(sem.cen, 1)
+    S.activation(out=xc[:, half:TK], in_=xc[:, half:TK], func=F.Identity, scale=rs).then_inc(sem.fy, 1)
+
+    Y.wait_ge(sem.fy, 2)
+    Y.dma_start(T.y[:], xc[:]).then_inc(sem.sto, 16)
+    Y.wait_ge(sem.sto, 16)
+    g.wait_ge(sem.snt, 2 * K_SEND)

@@ -1,3 +1,4 @@
+import math
 from concourse.bass import DstId, RemoteDMATransfer
 from concourse.mybir import AluOpType, AxisListType, ActivationFunctionType
 
@@ -6,8 +7,16 @@ NT = 4 * TK
 EPS = 0.01
 SIM_CORES = 512
 
-K_SEND = 4
+K_SEND = 8
 K_RELAY = 8
+
+J = 32
+H = 0.68
+U0 = 0.5 * math.log(EPS) - 4.0
+ULAST = U0 + (J - 1) * H
+QF = math.exp(-H)
+C = 2.0 * H / math.pi * math.exp(ULAST)
+TAIL_UP = math.exp(-(ULAST + H) - ULAST) / (1.0 - QF)
 
 SCRATCH = {
     "xs": ("sbuf", [128, TK], "float32"),
@@ -16,10 +25,14 @@ SCRATCH = {
     "part": ("sbuf", [128, 4], "float32"),
     "rem": ("sbuf", [128, 4], "float32"),
     "rl": ("sbuf", [128, 4], "float32"),
-    "pre": ("sbuf", [128, 4], "float32"),
-    "fin": ("sbuf", [128, 8], "float32"),
+    "pre": ("sbuf", [128, 8], "float32"),
+    "fin": ("sbuf", [128, 4], "float32"),
+    "ta": ("sbuf", [128, J], "float32"),
+    "d0": ("sbuf", [128, J + 4], "float32"),
+    "r": ("sbuf", [128, J + 4], "float32"),
+    "sc": ("sbuf", [128, J + 4], "float32"),
 }
-SEMAPHORES = ["ld", "stt", "pa", "ra", "rla", "snt", "pr", "f1", "mu", "cen", "sd", "rs", "fy", "sto"]
+SEMAPHORES = ["ld", "stt", "pa", "ra", "rla", "snt", "tb", "pr", "f1", "nm", "cen", "c1", "c2", "c3", "fy", "sto"]
 
 
 def _engines(allowed, k):
@@ -78,7 +91,9 @@ def rank_program(g, core, T, topo):
     relay, slot = [(r, sr[0].index(core)) for r, sr in relays.items() if core in sr[0]][0]
     partner = [c for c in T.cores if c != core and topo.host(c) == topo.host(core) and topo.chip(c) == topo.chip(core)][0]
     st, part, rem, pre, fin, xs, xc = T.st, T.part, T.rem, T.pre, T.fin, T.xs, T.xc
-    e2, mu, musq, sd, rs = (fin[:, i:i + 1] for i in range(5))
+    ta, d0, r, sc = T.ta, T.d0, T.r, T.sc
+    e2, musq, nmc = (fin[:, i:i + 1] for i in range(3))
+    s = sc[:, J:J + 1]
     half = TK // 2
 
     Y.dma_start(xs[:], T.x[:]).then_inc(sem.ld, 16)
@@ -95,34 +110,52 @@ def rank_program(g, core, T, topo):
     g.remote_dma(part[:, 0:2], st[:, 0:2], sem.pa, sem.snt, pid, rid,
                  _engines(topo.mask(core, partner) & topo.mask(core, relay), K_SEND))
 
+    V.memset(ta[:, 0:1], math.exp(2.0 * U0)).then_inc(sem.tb, 1)
+    V.memset(d0[:, 0:1], QF / (1.0 - QF)).then_inc(sem.tb, 1)
+    V.memset(d0[:, 1:J], QF).then_inc(sem.tb, 1)
+    V.memset(d0[:, J:J + 1], 1.0).then_inc(sem.tb, 1)
+    V.memset(r[:, J:J + 1], TAIL_UP).then_inc(sem.tb, 1)
+    n, w = 5, 1
+    while w < J:
+        V.wait_ge(sem.tb, n)
+        V.tensor_scalar(out=ta[:, w:2 * w], in0=ta[:, 0:w], scalar1=math.exp(2.0 * H * w), scalar2=None,
+                        op0=A.mult).then_inc(sem.tb, 1)
+        n, w = n + 1, 2 * w
+    V.wait_ge(sem.tb, n)
+
     V.wait_ge(sem.stt, 2)
     V.wait_ge(sem.pa, K_SEND)
     V.tensor_tensor(out=pre[:, 0:2], in0=st[:, 0:2], in1=part[:, 0:2], op=A.add).then_inc(sem.pr, 1)
     V.wait_ge(sem.pr, 1)
     V.tensor_scalar(out=pre[:, 2:3], in0=pre[:, 0:1], scalar1=1.0 / NT, scalar2=None, op0=A.mult).then_inc(sem.pr, 1)
     V.tensor_scalar(out=pre[:, 3:4], in0=pre[:, 1:2], scalar1=NT * EPS, scalar2=None, op0=A.add).then_inc(sem.pr, 1)
-    V.wait_ge(sem.pr, 3)
-    S.wait_ge(sem.pr, 3)
+    V.tensor_scalar(out=pre[:, 4:5], in0=pre[:, 0:1], scalar1=-C / NT, scalar2=None, op0=A.mult).then_inc(sem.pr, 1)
+    V.wait_ge(sem.pr, 4)
+    S.wait_ge(sem.stt, 2)
+    S.wait_ge(sem.pr, 4)
 
-    S.wait_ge(sem.ra, K_RELAY)
-    S.activation(out=musq, in_=rem[:, 0:1], func=F.Square, bias=pre[:, 2:3], scale=1.0 / NT).then_inc(sem.f1, 1)
     V.wait_ge(sem.ra, K_RELAY)
     V.tensor_scalar(out=e2, in0=rem[:, 1:2], scalar1=pre[:, 3:4], scalar2=1.0 / NT,
                     op0=A.add, op1=A.mult).then_inc(sem.f1, 1)
-    V.tensor_scalar(out=mu, in0=rem[:, 0:1], scalar1=pre[:, 0:1], scalar2=1.0 / NT,
-                    op0=A.add, op1=A.mult).then_inc(sem.mu, 1)
-    S.wait_ge(sem.f1, 2)
-    S.activation(out=sd, in_=musq, func=F.Sqrt, bias=e2, scale=-1.0).then_inc(sem.sd, 1)
-    V.wait_ge(sem.mu, 1)
-    V.tensor_scalar(out=xc[:], in0=xs[:], scalar1=mu, scalar2=None, op0=A.subtract).then_inc(sem.cen, 1)
-    V.wait_ge(sem.sd, 1)
-    V.reciprocal(out=rs, in_=sd).then_inc(sem.rs, 1)
-    V.wait_ge(sem.rs, 1)
+    V.wait_ge(sem.f1, 2)
+    V.tensor_scalar(out=r[:, 0:J], in0=ta[:], scalar1=musq, scalar2=e2, op0=A.subtract, op1=A.add).then_inc(sem.c1, 1)
+    V.wait_ge(sem.c1, 1)
+    V.reciprocal(out=r[:, 0:J], in_=r[:, 0:J]).then_inc(sem.c2, 1)
+    V.wait_ge(sem.c2, 1)
+    V.tensor_tensor_scan(out=sc[:, 0:J + 1], data0=d0[:, 0:J + 1], data1=r[:, 0:J + 1], initial=r[:, 0:1],
+                         op0=A.mult, op1=A.add).then_inc(sem.c3, 1)
+    V.wait_ge(sem.c3, 1)
     V.wait_ge(sem.cen, 1)
-    V.tensor_scalar(out=xc[:, 0:half], in0=xc[:, 0:half], scalar1=rs, scalar2=None, op0=A.mult).then_inc(sem.fy, 1)
-    S.wait_ge(sem.rs, 1)
+    V.tensor_scalar(out=xc[:, 0:half], in0=xc[:, 0:half], scalar1=s, scalar2=None, op0=A.mult).then_inc(sem.fy, 1)
+
+    S.wait_ge(sem.ra, K_RELAY)
+    S.activation(out=musq, in_=rem[:, 0:1], func=F.Square, bias=pre[:, 2:3], scale=1.0 / NT).then_inc(sem.f1, 1)
+    S.activation(out=nmc, in_=rem[:, 0:1], func=F.Identity, bias=pre[:, 4:5], scale=-C / NT).then_inc(sem.nm, 1)
+    S.wait_ge(sem.nm, 1)
+    S.activation(out=xc[:], in_=xs[:], func=F.Identity, bias=nmc, scale=C).then_inc(sem.cen, 1)
     S.wait_ge(sem.cen, 1)
-    S.activation(out=xc[:, half:TK], in_=xc[:, half:TK], func=F.Identity, scale=rs).then_inc(sem.fy, 1)
+    S.wait_ge(sem.c3, 1)
+    S.activation(out=xc[:, half:TK], in_=xc[:, half:TK], func=F.Identity, scale=s).then_inc(sem.fy, 1)
 
     Y.wait_ge(sem.fy, 2)
     Y.dma_start(T.y[:], xc[:]).then_inc(sem.sto, 16)

import math
from concourse.bass import DstId, RemoteDMATransfer
from concourse.mybir import AluOpType, AxisListType, ActivationFunctionType

TK = 256
NT = 4 * TK
EPS = 0.01
SIM_CORES = 512

K_SEND = 8
K_RELAY = 8

J = 32
H = 0.68
U0 = 0.5 * math.log(EPS) - 4.0
ULAST = U0 + (J - 1) * H
QF = math.exp(-H)
C = 2.0 * H / math.pi * math.exp(ULAST)
TAIL_UP = math.exp(-(ULAST + H) - ULAST) / (1.0 - QF)

SCRATCH = {
    "xs": ("sbuf", [128, TK], "float32"),
    "xc": ("sbuf", [128, TK], "float32"),
    "st": ("sbuf", [128, 4], "float32"),
    "part": ("sbuf", [128, 4], "float32"),
    "rem": ("sbuf", [128, 4], "float32"),
    "rl": ("sbuf", [128, 4], "float32"),
    "pre": ("sbuf", [128, 8], "float32"),
    "fin": ("sbuf", [128, 4], "float32"),
    "ta": ("sbuf", [128, J], "float32"),
    "d0": ("sbuf", [128, J + 4], "float32"),
    "r": ("sbuf", [128, J + 4], "float32"),
    "sc": ("sbuf", [128, J + 4], "float32"),
}
SEMAPHORES = ["ld", "stt", "pa", "ra", "rla", "snt", "tb", "pr", "f1", "nm", "cen", "c1", "c2", "c3", "fy", "sto"]


def _engines(allowed, k):
    bits = [b for b in range(allowed.bit_length()) if (allowed >> b) & 1]
    m = 0
    for b in bits[:k]:
        m |= 1 << b
    return m


def _plan(T, topo):
    per_host = topo.CORES_PER_HOST
    groups = {}
    for c in T.cores:
        groups.setdefault(topo.host(c), []).append(c)
    relays = {}
    for hs, snd in groups.items():
        for hd, rcv in groups.items():
            if hd == hs:
                continue
            place = snd[0] % per_host
            cands = [h * per_host + place for h in range(SIM_CORES // per_host) if h not in groups]
            cands = [c for c in cands
                     if all(topo.may_write(s, c) for s in snd) and all(topo.may_write(c, d) for d in rcv)]
            cands.sort(key=lambda c: topo.rack(topo.host(c)) != topo.rack(hs))
            relays[cands[0]] = (snd, rcv)
    return relays


def _relay_program(g, core, T, topo, snd, rcv):
    allowed = topo.mask(core, rcv[0])
    for d in rcv:
        allowed &= topo.mask(core, d)
    ids = []
    for d in rcv:
        rid, pid = topo.addr(d, core)
        ids.append(DstId(rid=rid, pnc=pid))
    g.wait_ge(T.sem.rla, K_SEND * len(snd))
    g.remote_dma_fused(
        [RemoteDMATransfer(dst_ids=ids, dma_engine_mask=_engines(allowed, K_RELAY), remote_sem=T.sem.ra,
                           srcs=[T.rl[:, 2 * i:2 * i + 2] for i in range(len(snd))],
                           dsts=[T.rem[:, 0:2] for _ in rcv], alu_op=1)],
        local_sem=T.sem.snt)
    g.wait_ge(T.sem.snt, K_RELAY)


def rank_program(g, core, T, topo):
    relays = _plan(T, topo)
    if core in relays:
        _relay_program(g, core, T, topo, *relays[core])
        return
    if T.rank_of(core) is None:
        return
    V, S, Y, sem = g.vector, g.scalar, g.sync, T.sem
    A, F = AluOpType, ActivationFunctionType
    relay, slot = [(r, sr[0].index(core)) for r, sr in relays.items() if core in sr[0]][0]
    partner = [c for c in T.cores if c != core and topo.host(c) == topo.host(core) and topo.chip(c) == topo.chip(core)][0]
    st, part, rem, pre, fin, xs, xc = T.st, T.part, T.rem, T.pre, T.fin, T.xs, T.xc
    ta, d0, r, sc = T.ta, T.d0, T.r, T.sc
    e2, musq, nmc = (fin[:, i:i + 1] for i in range(3))
    s = sc[:, J:J + 1]
    half = TK // 2

    Y.dma_start(xs[:], T.x[:]).then_inc(sem.ld, 16)
    V.wait_ge(sem.ld, 16)
    V.tensor_reduce(out=st[:, 0:1], in_=xs[:], axis=AxisListType.X, op=A.add).then_inc(sem.stt, 1)
    S.wait_ge(sem.ld, 16)
    S.activation(out=xc[:], in_=xs[:], func=F.Square, accum_out=st[:, 1:2]).then_inc(sem.stt, 1)

    g.wait_ge(sem.stt, 2)
    rid, pid = topo.addr(relay, core)
    g.remote_dma(T.rl[:, 2 * slot:2 * slot + 2], st[:, 0:2], sem.rla, sem.snt, pid, rid,
                 _engines(topo.mask(core, relay), K_SEND))
    rid, pid = topo.addr(partner, core)
    g.remote_dma(part[:, 0:2], st[:, 0:2], sem.pa, sem.snt, pid, rid,
                 _engines(topo.mask(core, partner) & topo.mask(core, relay), K_SEND))

    V.memset(ta[:, 0:1], math.exp(2.0 * U0)).then_inc(sem.tb, 1)
    V.memset(d0[:, 0:1], QF / (1.0 - QF)).then_inc(sem.tb, 1)
    V.memset(d0[:, 1:J], QF).then_inc(sem.tb, 1)
    V.memset(d0[:, J:J + 1], 1.0).then_inc(sem.tb, 1)
    V.memset(r[:, J:J + 1], TAIL_UP).then_inc(sem.tb, 1)
    n, w = 5, 1
    while w < J:
        V.wait_ge(sem.tb, n)
        V.tensor_scalar(out=ta[:, w:2 * w], in0=ta[:, 0:w], scalar1=math.exp(2.0 * H * w), scalar2=None,
                        op0=A.mult).then_inc(sem.tb, 1)
        n, w = n + 1, 2 * w
    V.wait_ge(sem.tb, n)

    V.wait_ge(sem.stt, 2)
    V.wait_ge(sem.pa, K_SEND)
    V.tensor_tensor(out=pre[:, 0:2], in0=st[:, 0:2], in1=part[:, 0:2], op=A.add).then_inc(sem.pr, 1)
    V.wait_ge(sem.pr, 1)
    V.tensor_scalar(out=pre[:, 2:3], in0=pre[:, 0:1], scalar1=1.0 / NT, scalar2=None, op0=A.mult).then_inc(sem.pr, 1)
    V.tensor_scalar(out=pre[:, 3:4], in0=pre[:, 1:2], scalar1=NT * EPS, scalar2=None, op0=A.add).then_inc(sem.pr, 1)
    V.tensor_scalar(out=pre[:, 4:5], in0=pre[:, 0:1], scalar1=-C / NT, scalar2=None, op0=A.mult).then_inc(sem.pr, 1)
    V.wait_ge(sem.pr, 4)
    S.wait_ge(sem.stt, 2)
    S.wait_ge(sem.pr, 4)

    V.wait_ge(sem.ra, K_RELAY)
    V.tensor_scalar(out=e2, in0=rem[:, 1:2], scalar1=pre[:, 3:4], scalar2=1.0 / NT,
                    op0=A.add, op1=A.mult).then_inc(sem.f1, 1)
    V.wait_ge(sem.f1, 2)
    V.tensor_scalar(out=r[:, 0:J], in0=ta[:], scalar1=musq, scalar2=e2, op0=A.subtract, op1=A.add).then_inc(sem.c1, 1)
    V.wait_ge(sem.c1, 1)
    V.reciprocal(out=r[:, 0:J], in_=r[:, 0:J]).then_inc(sem.c2, 1)
    V.wait_ge(sem.c2, 1)
    V.tensor_tensor_scan(out=sc[:, 0:J + 1], data0=d0[:, 0:J + 1], data1=r[:, 0:J + 1], initial=r[:, 0:1],
                         op0=A.mult, op1=A.add).then_inc(sem.c3, 1)
    V.wait_ge(sem.c3, 1)
    V.wait_ge(sem.cen, 1)
    V.tensor_scalar(out=xc[:, 0:half], in0=xc[:, 0:half], scalar1=s, scalar2=None, op0=A.mult).then_inc(sem.fy, 1)

    S.wait_ge(sem.ra, K_RELAY)
    S.activation(out=musq, in_=rem[:, 0:1], func=F.Square, bias=pre[:, 2:3], scale=1.0 / NT).then_inc(sem.f1, 1)
    S.activation(out=nmc, in_=rem[:, 0:1], func=F.Identity, bias=pre[:, 4:5], scale=-C / NT).then_inc(sem.nm, 1)
    S.wait_ge(sem.nm, 1)
    S.activation(out=xc[:], in_=xs[:], func=F.Identity, bias=nmc, scale=C).then_inc(sem.cen, 1)
    S.wait_ge(sem.cen, 1)
    S.wait_ge(sem.c3, 1)
    S.activation(out=xc[:, half:TK], in_=xc[:, half:TK], func=F.Identity, scale=s).then_inc(sem.fy, 1)

    Y.wait_ge(sem.fy, 2)
    Y.dma_start(T.y[:], xc[:]).then_inc(sem.sto, 16)
    Y.wait_ge(sem.sto, 16)
    g.wait_ge(sem.snt, 2 * K_SEND)
